import numpy as np
import ml_dtypes


def mxq(x, axis, fmt="e4m3"):
    dtype, down = {"e4m3": (ml_dtypes.float8_e4m3fn, 7), "e5m2": (ml_dtypes.float8_e5m2, 14)}[fmt]
    v = np.moveaxis(np.asarray(x, np.float32).astype(ml_dtypes.bfloat16).astype(np.float64), axis, -1)
    blocks = v.reshape(v.shape[:-1] + (-1, 32))
    amax = np.abs(blocks).max(-1, keepdims=True)
    byte = np.maximum(np.where(amax > 0, np.frexp(amax)[1] - 1 + 127, 0) - down, 1)
    scale = np.exp2(byte - 127.0)
    codes = (blocks / scale).astype(np.float32).astype(dtype).astype(np.float64)
    return np.moveaxis((codes * scale).reshape(v.shape), -1, axis)


WIDE = False


def mx_kscale(k):
    if not WIDE:
        return np.ones(k)
    levels = np.array([10, -10, 5, -5, 0])
    if k % 512:
        return np.exp2(np.random.permutation(np.resize(levels, k // 32))).repeat(32)
    a = np.empty((k // 512, 16))
    for p in range(k // 512):
        a[p, :8] = np.random.permutation(np.resize(levels, 8))
        for g in range(8):
            far = levels[np.abs(levels - a[p, g]) >= 10]
            a[p, g + 8] = far[np.random.randint(len(far))]
    return np.exp2(a.ravel()).repeat(32)


def f64(x):
    return np.asarray(x).astype(np.float64)


def striped(idx):
    return np.tile(np.asarray(idx).reshape(-1, 16).T, (8, 1)).astype(np.uint16)


def unstriped(offs):
    return offs[:16].T.reshape(-1).astype(np.int64)


E2M1 = np.array([0.0, 0.5, 1.0, 1.5, 2.0, 3.0, 4.0, 6.0, -0.0, -0.5, -1.0, -1.5, -2.0, -3.0, -4.0, -6.0])


def pack_weight(w, fmt):
    k, n = w.shape
    w = f64(np.asarray(w, np.float32).astype(ml_dtypes.bfloat16)).reshape(k // 32, 32, n)
    amax = np.abs(w).max(1)
    if fmt == "e4m3":
        byte = np.frexp(amax)[1] - 1 + 127 - 7
    else:
        mant, ex = np.frexp(amax / 6.0)
        byte = np.where(mant > 0.5, ex, ex - 1) + 127
    byte = np.clip(np.where(amax > 0, byte, 1), 1, 254)
    scaled = (w * np.exp2(127.0 - byte)[:, None, :]).reshape(k, n).astype(np.float32)
    by_word = np.ascontiguousarray(scaled.reshape(k // 512, 128, 4, n).transpose(0, 1, 3, 2))
    if fmt == "e4m3":
        words = by_word.astype(ml_dtypes.float8_e4m3fn).view(np.uint8)
    else:
        c = by_word.astype(ml_dtypes.float4_e2m1fn).view(np.uint8) & 0xF
        words = (c[..., 0::2] | (c[..., 1::2] << 4)).reshape(k // 512, 128, 2 * n)
    return np.ascontiguousarray(words), np.ascontiguousarray(byte.astype(np.uint8).reshape(k // 512, 16, n))


def unpack_weight(words, scales, fmt):
    g, _, n = scales.shape
    words = np.ascontiguousarray(words).reshape(g, 128, n, -1)
    if fmt == "e4m3":
        vals = words.view(ml_dtypes.float8_e4m3fn).astype(np.float64)
    else:
        nib = np.empty((g, 128, n, 4), np.uint8)
        nib[..., 0::2] = words & 0xF
        nib[..., 1::2] = words >> 4
        vals = E2M1[nib]
    vals = vals * np.repeat(np.exp2(scales.astype(np.float64) - 127.0), 8, axis=1)[..., None]
    return vals.transpose(0, 1, 3, 2).reshape(g * 512, n)


D, T, I, Q, E, Z, C = 512, 2048, 512, 512, 512, 1024, 256


def setup_inputs():
    n = np.random.standard_normal
    idx = np.random.permutation(T)[:I]
    idx2 = np.random.permutation(Z)[:I]
    idx3 = np.random.permutation(Z)[:I]
    idx4 = np.random.permutation(Q)[:C]
    fd = mx_kscale(D)
    fi = mx_kscale(I)
    ti = np.ones(T)
    ti[idx] = fi
    keysp = pack_weight(n((D, T)) / fd[:, None], "e4m3")
    return {
        "query": (n((D, Q)) * 1.0 / np.sqrt(D) * fd[:, None]).astype(np.float32),
        "keys_words": keysp[0],
        "keys_scales": keysp[1],
        "os": (np.random.uniform(0.02, 0.08, (1, I)) * fi).astype(np.float32),
        "vals": (n((E, T)) / ti).astype(np.float32),
        "pgain": (np.random.uniform(0.5, 2.0, (1, C))).astype(np.float32),
        "offs": striped(idx),
        "offs2": striped(idx2),
        "offs3": striped(idx3),
        "offs4": striped(idx4),
    }


def reference(query, keys_words, keys_scales, os, vals, pgain, offs, offs2, offs3, offs4):
    idx = unstriped(offs)
    idx2 = unstriped(offs2)
    idx3 = unstriped(offs3)
    idx4 = unstriped(offs4)
    keysu = unpack_weight(keys_words, keys_scales, "e4m3")
    queryq = mxq(f64(query), 0, "e4m3")
    keysidxg = keysu[:, idx]
    a = queryq.T @ keysidxg
    f0 = np.zeros((Q, Z))
    f0[:, idx2] = a
    s = a + f0[:, idx3]
    w = np.maximum(s, 0.0)
    wo1 = w * f64(os)
    wt1 = wo1.T
    vt1 = f64(vals)[:, idx].T
    vt1q = mxq(vt1, 0, "e4m3")
    wt1q = mxq(wt1, 0, "e4m3")
    o = vt1q.T @ wt1q
    y = o[:, idx4] * f64(pgain)
    return y

@@ -1,0 +1,295 @@
+from contextlib import ExitStack
+
+import concourse.mybir as mybir
+from concourse.masks import make_identity
+
+D, T, I, Q, E, Z, C = 512, 2048, 512, 512, 512, 1024, 256
+FLOPS = 2 * D * Q * I + 2 * I * E * Q
+
+F32 = mybir.dt.float32
+BF16 = mybir.dt.bfloat16
+I32 = mybir.dt.int32
+U32 = mybir.dt.uint32
+U16 = mybir.dt.uint16
+U8 = mybir.dt.uint8
+FP8X4 = mybir.dt.float8_e4m3fn_x4
+COPY = mybir.ActivationFunctionType.Copy
+MAX = mybir.AluOpType.max
+MULT = mybir.AluOpType.mult
+
+P = 128
+PACK = 4
+BLOCKS = Q // P
+PLANES = E // P
+HALF = I // 2
+
+
+def tile_attend_passedthrough_pickedout_lean_kernel(
+    tc, query, keys_words, keys_scales, slot_factor, vals, pgain, offs, offs2, offs3, offs4, out
+):
+    nc = tc.nc
+    with ExitStack() as ctx:
+        keep = ctx.enter_context(tc.tile_pool(name="keep", bufs=1))
+        psum = ctx.enter_context(tc.psum_pool(name="psum", bufs=1))
+
+        def tiles(name, count, shape, dtype):
+            return [keep.tile(shape, dtype, name="%s%d" % (name, n), tag="%s%d" % (name, n), align_bytes=64) for n in range(count)]
+
+        token_list = keep.tile([P, I // 16], U16)
+        put_list = keep.tile([P, I // 16], U16)
+        get_list = keep.tile([P, I // 16], U16)
+        column_list = keep.tile([P, C // 16], U16)
+        pool_words = keep.tile([P, T], U32, align_bytes=64)
+        pool_scales = keep.tile([P, T], U8, align_bytes=64)
+        key_words = keep.tile([P, I], U32, align_bytes=64)
+        key_scales = keep.tile([P, I], U8, align_bytes=64)
+        query_raw = tiles("query_raw", 2, [P, PACK, P], F32)
+        query_late = keep.tile([P, PACK, 2 * P], F32)
+        query_bf = tiles("query_bf", BLOCKS, [P, P, PACK], BF16)
+        query_words = tiles("query_words", BLOCKS, [P, P], U32)
+        query_scales = tiles("query_scales", BLOCKS, [P, P], U8)
+        products = tiles("products", BLOCKS, [P, I], F32)
+        places = tiles("places", 2, [P, Z], F32)
+        looked_up = {}
+        weights_bf = {}
+        value_banks = {}
+        weight_words = keep.tile([P, Q], U32, align_bytes=64)
+        weight_scales = keep.tile([P, Q], U8, align_bytes=64)
+        value_pool = tiles("value_pool", PLANES, [P, T], F32)
+        picked = tiles("picked", PLANES, [P, I], BF16)
+        values_bf = tiles("values_bf", PLANES // 2, [P, 2, P, PACK], BF16)
+        value_words = tiles("value_words", PLANES // 2, [P, 2 * P], U32)
+        value_scales = tiles("value_scales", PLANES // 2, [P, 2 * P], U8)
+        sums = []
+        sum_tags = ["value_pool3", "picked3", "sums2", "sums3"]
+        result = tiles("result", PLANES, [P, C], F32)
+        columns = keep.tile([P, C], F32)
+        factor = keep.tile([P, PACK], F32)
+        gain = keep.tile([P, C], F32)
+        identity = keep.tile([P, P], F32, tag="identity", align_bytes=64)
+
+        nc.vector.memset(pool_scales[:].bitcast(I32), 0)
+        for window in places:
+            nc.vector.memset(window[:], 0.0)
+        make_identity(nc, identity[:])
+
+        query_rows = query.rearrange("(p j) q -> p j q", j=PACK)
+        value_rows = vals.rearrange("(p j) t -> p j t", j=PLANES)
+        out_rows = out.rearrange("(p j) c -> p j c", j=PLANES)
+
+        nc.sync.dma_start(token_list[:], offs)
+        nc.sync.dma_start(pool_words[:].bitcast(I32), keys_words[0].rearrange("p n r -> p (n r)").bitcast(I32))
+        for quadrant in range(4):
+            nc.sync.dma_start(
+                pool_scales[:].bitcast(I32)[32 * quadrant : 32 * quadrant + 4, :],
+                keys_scales[0].bitcast(I32)[4 * quadrant : 4 * quadrant + 4, :],
+            )
+        nc.sync.dma_start(query_raw[0][:], query_rows[:, :, 0:P])
+        nc.sync.dma_start(query_raw[1][:], query_rows[:, :, P : 2 * P])
+        nc.sync.dma_start(put_list[:], offs2)
+        nc.sync.dma_start(query_late[:], query_rows[:, :, 2 * P :])
+        nc.sync.dma_start(get_list[:], offs3)
+        nc.sync.dma_start(factor[:], slot_factor[0].rearrange("(p r) -> p r", r=PACK))
+        for j in range(PLANES):
+            nc.sync.dma_start(value_pool[j][:], value_rows[:, j, :])
+        nc.sync.dma_start(column_list[:], offs4)
+        nc.sync.dma_start(gain[:], pgain[0].partition_broadcast(P))
+
+        def interleave_query(b, on_scalar):
+            dst = query_bf[b][:].rearrange("p (c n) r -> p c r n", n=4)
+            raw = query_raw[b][:] if b < 2 else query_late[:, :, (b - 2) * P : (b - 1) * P]
+            src = raw.rearrange("p r (c n) -> p c r n", n=4)
+            if on_scalar:
+                nc.scalar.activation(dst, src, COPY)
+            else:
+                nc.vector.tensor_copy(dst, src)
+
+        def quantise_query(b):
+            nc.vector.quantize_mx(
+                out=query_words[b][:].bitcast(FP8X4),
+                scales=query_scales[b][:],
+                in_=query_bf[b][:].rearrange("p q r -> p (q r)"),
+            )
+
+        def gather_keys(h):
+            nc.vector.tensor_copy(
+                key_words[:, h * HALF : (h + 1) * HALF], pool_words[:].indirect(token_list[:, h * 16 : (h + 1) * 16])
+            )
+            nc.vector.tensor_copy(
+                key_scales[:, h * HALF : (h + 1) * HALF], pool_scales[:].indirect(token_list[:, h * 16 : (h + 1) * 16])
+            )
+
+        def score(b, cols, on_scalar, bank_tag):
+            bank = psum.tile([P, cols.stop - cols.start], F32, name="product_bank", tag=bank_tag)
+            nc.tensor.matmul_mx(
+                out=bank[:],
+                lhsT=query_words[b][:].bitcast(FP8X4),
+                lhsT_scale=query_scales[b][:],
+                rhs=key_words[:, cols].bitcast(FP8X4),
+                rhs_scale=key_scales[:, cols],
+                start=True,
+                stop=True,
+            )
+            if on_scalar:
+                nc.scalar.copy(products[b][:, cols], bank[:])
+            else:
+                nc.vector.tensor_copy(products[b][:, cols], bank[:])
+
+        score_banks = [psum.tile([P, PACK, P], F32, name="score_bank%d" % b, tag="score%d" % b) for b in range(BLOCKS)]
+
+        def turn(b, source, first):
+            for r in range(PACK):
+                nc.tensor.matmul(
+                    score_banks[b][:, r, :],
+                    lhsT=source[:, r::PACK],
+                    rhs=identity[:],
+                    is_transpose=True,
+                    start=first and r == 0,
+                    stop=not first and r == PACK - 1,
+                )
+
+        def put_half(b, h):
+            nc.scalar.activation(
+                places[b % 2][:].indirect(put_list[:, h * 16 : (h + 1) * 16]),
+                products[b][:, h * HALF : (h + 1) * HALF],
+                COPY,
+            )
+
+        def put(b):
+            nc.vector.tensor_copy(places[b % 2][:].indirect(put_list[:]), products[b][:])
+
+        def get(b, on_scalar):
+            window = places[b % 2][:].indirect(get_list[:])
+            tag = "value_pool1" if b == 2 else "looked_up%d" % b
+            looked_up[b] = keep.tile([P, I], F32, name="looked_up%d" % b, tag=tag, align_bytes=64)
+            if on_scalar:
+                nc.scalar.activation(looked_up[b][:], window, COPY)
+            else:
+                nc.vector.tensor_copy(looked_up[b][:], window)
+            turn(b, looked_up[b], False)
+
+        def weigh(b):
+            if b // 2 not in weights_bf:
+                tag = "products3" if b < 2 else "weights_late"
+                weights_bf[b // 2] = keep.tile([P, 2 * P, PACK], BF16, name="weights_bf", tag=tag, align_bytes=64)
+            nc.vector.scalar_tensor_tensor(
+                out=weights_bf[b // 2][:, (b % 2) * P : (b % 2 + 1) * P, :],
+                in0=score_banks[b][:].rearrange("p r q -> p q r"),
+                scalar=0.0,
+                in1=factor[:].unsqueeze(1).to_broadcast([P, P, PACK]),
+                op0=MAX,
+                op1=MULT,
+            )
+
+        def quantise_weights(h):
+            cols = slice(h * 2 * P, (h + 1) * 2 * P)
+            nc.vector.quantize_mx(
+                out=weight_words[:, cols].bitcast(FP8X4),
+                scales=weight_scales[:, cols],
+                in_=weights_bf[h][:].rearrange("p q r -> p (q r)"),
+            )
+
+        def pick(j, on_scalar):
+            window = value_pool[j][:].indirect(token_list[:])
+            if on_scalar:
+                nc.scalar.activation(picked[j][:], window, COPY)
+            else:
+                nc.vector.tensor_copy(picked[j][:], window)
+            pairs = picked[j][:].bitcast(F32)
+            if j % 2 == 0:
+                value_banks[j // 2] = psum.tile([P, 2, 2, P], F32, name="value_bank", tag="mx%d" % (j // 2))
+            for u in range(2):
+                nc.tensor.transpose(value_banks[j // 2][:, j % 2, u, :], pairs[:, u::2], identity[:])
+
+        def lay_values(g, on_scalar):
+            dst = values_bf[g][:].bitcast(F32)
+            src = value_banks[g][:].rearrange("p j u e -> p j e u")
+            if on_scalar:
+                nc.scalar.copy(dst, src)
+            else:
+                nc.vector.tensor_copy(dst, src)
+
+        def quantise_values(g):
+            nc.vector.quantize_mx(
+                out=value_words[g][:].bitcast(FP8X4),
+                scales=value_scales[g][:],
+                in_=values_bf[g][:].rearrange("p j e r -> p (j e r)"),
+            )
+
+        def add_up(j):
+            cols = slice((j % 2) * P, (j % 2 + 1) * P)
+            bank = psum.tile([P, Q], F32, name="sum_bank", tag=["mx2", "mx3", "score0", "score1"][j])
+            nc.tensor.matmul_mx(
+                out=bank[:],
+                lhsT=value_words[j // 2][:, cols].bitcast(FP8X4),
+                lhsT_scale=value_scales[j // 2][:, cols],
+                rhs=weight_words[:].bitcast(FP8X4),
+                rhs_scale=weight_scales[:],
+                start=True,
+                stop=True,
+            )
+            sums.append(keep.tile([P, Q], F32, name="sums%d" % j, tag=sum_tags[j], align_bytes=64))
+            nc.scalar.copy(sums[j][:], bank[:])
+
+        def give_out(j, on_scalar):
+            window = sums[j][:].indirect(column_list[:])
+            if on_scalar:
+                nc.scalar.activation(columns[:], window, COPY)
+                nc.vector.tensor_tensor(result[j][:], columns[:], gain[:], MULT)
+            else:
+                nc.vector.tensor_tensor(result[j][:], window, gain[:], MULT)
+            nc.sync.dma_start(out_rows[:, j, :], result[j][:])
+
+
+        whole = slice(0, I)
+        gather_keys(0)
+        interleave_query(0, True)
+        quantise_query(0)
+        score(0, slice(0, HALF), True, "mx2")
+        gather_keys(1)
+        interleave_query(1, True)
+        put_half(0, 0)
+        score(0, slice(HALF, I), True, "mx0")
+        quantise_query(1)
+        interleave_query(2, False)
+        score(1, whole, False, "mx1")
+        interleave_query(3, False)
+        quantise_query(2)
+        quantise_query(3)
+        score(2, whole, True, "mx2")
+        put(1)
+        score(3, whole, False, "mx3")
+        put_half(0, 1)
+        turn(0, products[0], True)
+        turn(1, products[1], True)
+        pick(0, True)
+        get(0, True)
+        get(1, False)
+        turn(2, products[2], True)
+        turn(3, products[3], True)
+        put_half(2, 0)
+        put(3)
+        put_half(2, 1)
+        pick(1, True)
+        get(3, False)
+        get(2, True)
+        weigh(0)
+        weigh(1)
+        pick(2, True)
+        quantise_weights(0)
+        lay_values(0, False)
+        weigh(3)
+        quantise_values(0)
+        weigh(2)
+        quantise_weights(1)
+        pick(3, True)
+        lay_values(1, True)
+        add_up(0)
+        add_up(1)
+        quantise_values(1)
+        give_out(0, False)
+        add_up(2)
+        give_out(1, False)
+        add_up(3)
+        give_out(2, False)
+        give_out(3, True)

@@ -43,32 +43,33 @@ def tile_attend_passedthrough_pickedout_lean_kernel(
         pool_scales = keep.tile([P, T], U8, align_bytes=64)
         key_words = keep.tile([P, I], U32, align_bytes=64)
         key_scales = keep.tile([P, I], U8, align_bytes=64)
-        query_raw = tiles("query_raw", 2, [P, PACK, P], F32)
-        query_late = keep.tile([P, PACK, 2 * P], F32)
-        query_bf = tiles("query_bf", BLOCKS, [P, P, PACK], BF16)
-        query_words = tiles("query_words", BLOCKS, [P, P], U32)
-        query_scales = tiles("query_scales", BLOCKS, [P, P], U8)
+        widths = [P, P, 2 * P]
+        query_raw = [keep.tile([P, PACK, w], F32, name="query_raw%d" % n) for n, w in enumerate(widths)]
+        query_bf = [keep.tile([P, w, PACK], BF16, name="query_bf%d" % n, align_bytes=64) for n, w in enumerate(widths)]
+        query_words = [keep.tile([P, w], U32, name="query_words%d" % n, align_bytes=64) for n, w in enumerate(widths)]
+        query_scales = [keep.tile([P, w], U8, name="query_scales%d" % n, align_bytes=64) for n, w in enumerate(widths)]
         products = tiles("products", BLOCKS, [P, I], F32)
         places = tiles("places", 2, [P, Z], F32)
         looked_up = {}
         weights_bf = {}
         value_banks = {}
-        weight_words = keep.tile([P, Q], U32, align_bytes=64)
-        weight_scales = keep.tile([P, Q], U8, align_bytes=64)
+        weight_words = {}
+        weight_scales = tiles("weight_scales", 2, [P, HALF], U8)
         value_pool = tiles("value_pool", PLANES, [P, T], F32)
         picked = tiles("picked", PLANES, [P, I], BF16)
         values_bf = tiles("values_bf", PLANES // 2, [P, 2, P, PACK], BF16)
         value_words = tiles("value_words", PLANES // 2, [P, 2 * P], U32)
         value_scales = tiles("value_scales", PLANES // 2, [P, 2 * P], U8)
-        sums = []
-        sum_tags = ["value_pool3", "picked3", "sums2", "sums3"]
+        sums = tiles("sums", PLANES, [P, Q], F32)
+        sum_banks = {}
         result = tiles("result", PLANES, [P, C], F32)
         columns = keep.tile([P, C], F32)
         factor = keep.tile([P, PACK], F32)
         gain = keep.tile([P, C], F32)
         identity = keep.tile([P, P], F32, tag="identity", align_bytes=64)
 
-        nc.vector.memset(pool_scales[:].bitcast(I32), 0)
+        nc.vector.memset(pool_scales[:].bitcast(I32)[:, 0 : T // 8], 0)
+        nc.gpsimd.memset(pool_scales[:].bitcast(I32)[:, T // 8 :], 0)
         for window in places:
             nc.vector.memset(window[:], 0.0)
         make_identity(nc, identity[:])
@@ -78,16 +79,16 @@ def tile_attend_passedthrough_pickedout_lean_kernel(
         out_rows = out.rearrange("(p j) c -> p j c", j=PLANES)
 
         nc.sync.dma_start(token_list[:], offs)
-        nc.sync.dma_start(pool_words[:].bitcast(I32), keys_words[0].rearrange("p n r -> p (n r)").bitcast(I32))
+        nc.sync.dma_start(query_raw[0][:], query_rows[:, :, 0:P])
+        nc.sync.dma_start(put_list[:], offs2)
         for quadrant in range(4):
             nc.sync.dma_start(
                 pool_scales[:].bitcast(I32)[32 * quadrant : 32 * quadrant + 4, :],
                 keys_scales[0].bitcast(I32)[4 * quadrant : 4 * quadrant + 4, :],
             )
-        nc.sync.dma_start(query_raw[0][:], query_rows[:, :, 0:P])
+        nc.sync.dma_start(pool_words[:].bitcast(I32), keys_words[0].rearrange("p n r -> p (n r)").bitcast(I32))
         nc.sync.dma_start(query_raw[1][:], query_rows[:, :, P : 2 * P])
-        nc.sync.dma_start(put_list[:], offs2)
-        nc.sync.dma_start(query_late[:], query_rows[:, :, 2 * P :])
+        nc.sync.dma_start(query_raw[2][:], query_rows[:, :, 2 * P :])
         nc.sync.dma_start(get_list[:], offs3)
         nc.sync.dma_start(factor[:], slot_factor[0].rearrange("(p r) -> p r", r=PACK))
         for j in range(PLANES):
@@ -97,8 +98,7 @@ def tile_attend_passedthrough_pickedout_lean_kernel(
 
         def interleave_query(b, on_scalar):
             dst = query_bf[b][:].rearrange("p (c n) r -> p c r n", n=4)
-            raw = query_raw[b][:] if b < 2 else query_late[:, :, (b - 2) * P : (b - 1) * P]
-            src = raw.rearrange("p r (c n) -> p c r n", n=4)
+            src = query_raw[b][:].rearrange("p r (c n) -> p c r n", n=4)
             if on_scalar:
                 nc.scalar.activation(dst, src, COPY)
             else:
@@ -115,16 +115,15 @@ def tile_attend_passedthrough_pickedout_lean_kernel(
             nc.vector.tensor_copy(
                 key_words[:, h * HALF : (h + 1) * HALF], pool_words[:].indirect(token_list[:, h * 16 : (h + 1) * 16])
             )
-            nc.vector.tensor_copy(
-                key_scales[:, h * HALF : (h + 1) * HALF], pool_scales[:].indirect(token_list[:, h * 16 : (h + 1) * 16])
-            )
 
         def score(b, cols, on_scalar, bank_tag):
             bank = psum.tile([P, cols.stop - cols.start], F32, name="product_bank", tag=bank_tag)
+            piece = min(b, 2)
+            rows = slice((b - piece) * P, (b - piece + 1) * P)
             nc.tensor.matmul_mx(
                 out=bank[:],
-                lhsT=query_words[b][:].bitcast(FP8X4),
-                lhsT_scale=query_scales[b][:],
+                lhsT=query_words[piece][:, rows].bitcast(FP8X4),
+                lhsT_scale=query_scales[piece][:, rows],
                 rhs=key_words[:, cols].bitcast(FP8X4),
                 rhs_scale=key_scales[:, cols],
                 start=True,
@@ -182,54 +181,65 @@ def tile_attend_passedthrough_pickedout_lean_kernel(
             )
 
         def quantise_weights(h):
-            cols = slice(h * 2 * P, (h + 1) * 2 * P)
+            tag = "picked3" if h == 1 else "weight_words"
+            weight_words[h] = keep.tile([P, HALF], U32, name="weight_words", tag=tag, align_bytes=64)
             nc.vector.quantize_mx(
-                out=weight_words[:, cols].bitcast(FP8X4),
-                scales=weight_scales[:, cols],
+                out=weight_words[h][:].bitcast(FP8X4),
+                scales=weight_scales[h][:],
                 in_=weights_bf[h][:].rearrange("p q r -> p (q r)"),
             )
 
-        def pick(j, on_scalar):
-            window = value_pool[j][:].indirect(token_list[:])
+        def pick(j, cols, on_scalar):
+            window = value_pool[j][:].indirect(token_list[:, cols.start // 16 : cols.stop // 16])
             if on_scalar:
-                nc.scalar.activation(picked[j][:], window, COPY)
+                nc.scalar.activation(picked[j][:, cols], window, COPY)
             else:
-                nc.vector.tensor_copy(picked[j][:], window)
+                nc.vector.tensor_copy(picked[j][:, cols], window)
+
+        def turn_values(j):
             pairs = picked[j][:].bitcast(F32)
             if j % 2 == 0:
                 value_banks[j // 2] = psum.tile([P, 2, 2, P], F32, name="value_bank", tag="mx%d" % (j // 2))
             for u in range(2):
                 nc.tensor.transpose(value_banks[j // 2][:, j % 2, u, :], pairs[:, u::2], identity[:])
 
-        def lay_values(g, on_scalar):
-            dst = values_bf[g][:].bitcast(F32)
-            src = value_banks[g][:].rearrange("p j u e -> p j e u")
+        def lay_values(planes, on_scalar):
+            g, part = planes.start // 2, slice(planes.start % 2, (planes.stop - 1) % 2 + 1)
+            dst = values_bf[g][:, part].bitcast(F32)
+            src = value_banks[g][:, part].rearrange("p j u e -> p j e u")
             if on_scalar:
                 nc.scalar.copy(dst, src)
             else:
                 nc.vector.tensor_copy(dst, src)
 
-        def quantise_values(g):
+        def quantise_values(planes):
+            g, part = planes.start // 2, slice(planes.start % 2, (planes.stop - 1) % 2 + 1)
+            cols = slice(part.start * P, part.stop * P)
             nc.vector.quantize_mx(
-                out=value_words[g][:].bitcast(FP8X4),
-                scales=value_scales[g][:],
-                in_=values_bf[g][:].rearrange("p j e r -> p (j e r)"),
+                out=value_words[g][:, cols].bitcast(FP8X4),
+                scales=value_scales[g][:, cols],
+                in_=values_bf[g][:, part].rearrange("p j e r -> p (j e r)"),
             )
 
-        def add_up(j):
+        def add_up(j, h):
             cols = slice((j % 2) * P, (j % 2 + 1) * P)
-            bank = psum.tile([P, Q], F32, name="sum_bank", tag=["mx2", "mx3", "score0", "score1"][j])
+            if j not in sum_banks:
+                sum_banks[j] = psum.tile([P, Q], F32, name="sum_bank", tag=["mx2", "mx3", "score0", "score1"][j])
             nc.tensor.matmul_mx(
-                out=bank[:],
+                out=sum_banks[j][:, h * HALF : (h + 1) * HALF],
                 lhsT=value_words[j // 2][:, cols].bitcast(FP8X4),
                 lhsT_scale=value_scales[j // 2][:, cols],
-                rhs=weight_words[:].bitcast(FP8X4),
-                rhs_scale=weight_scales[:],
+                rhs=weight_words[h][:].bitcast(FP8X4),
+                rhs_scale=weight_scales[h][:],
                 start=True,
                 stop=True,
             )
-            sums.append(keep.tile([P, Q], F32, name="sums%d" % j, tag=sum_tags[j], align_bytes=64))
-            nc.scalar.copy(sums[j][:], bank[:])
+
+        def copy_sums(j, on_scalar):
+            if on_scalar:
+                nc.scalar.copy(sums[j][:], sum_banks[j][:])
+            else:
+                nc.vector.tensor_copy(sums[j][:], sum_banks[j][:])
 
         def give_out(j, on_scalar):
             window = sums[j][:].indirect(column_list[:])
@@ -241,55 +251,64 @@ def tile_attend_passedthrough_pickedout_lean_kernel(
             nc.sync.dma_start(out_rows[:, j, :], result[j][:])
 
 
-        whole = slice(0, I)
-        gather_keys(0)
+        whole, early, late = slice(0, I), slice(0, HALF), slice(HALF, I)
         interleave_query(0, True)
         quantise_query(0)
-        score(0, slice(0, HALF), True, "mx2")
+        nc.vector.tensor_copy(key_scales[:], pool_scales[:].indirect(token_list[:]))
+        gather_keys(0)
+        score(0, early, True, "mx2")
         gather_keys(1)
         interleave_query(1, True)
         put_half(0, 0)
-        score(0, slice(HALF, I), True, "mx0")
+        score(0, late, True, "mx0")
         quantise_query(1)
         interleave_query(2, False)
         score(1, whole, False, "mx1")
-        interleave_query(3, False)
         quantise_query(2)
-        quantise_query(3)
-        score(2, whole, True, "mx2")
+        score(2, whole, False, "mx2")
         put(1)
         score(3, whole, False, "mx3")
         put_half(0, 1)
-        turn(0, products[0], True)
-        turn(1, products[1], True)
-        pick(0, True)
+        for b in range(BLOCKS):
+            turn(b, products[b], True)
+        pick(0, whole, True)
+        turn_values(0)
         get(0, True)
         get(1, False)
-        turn(2, products[2], True)
-        turn(3, products[3], True)
         put_half(2, 0)
         put(3)
         put_half(2, 1)
-        pick(1, True)
+        pick(1, whole, True)
+        turn_values(1)
         get(3, False)
         get(2, True)
         weigh(0)
         weigh(1)
-        pick(2, True)
+        pick(2, whole, True)
+        turn_values(2)
+        pick(3, whole, True)
+        turn_values(3)
         quantise_weights(0)
-        lay_values(0, False)
+        lay_values(slice(0, 2), False)
         weigh(3)
-        quantise_values(0)
+        quantise_values(slice(0, 2))
+        add_up(0, 0)
+        add_up(1, 0)
         weigh(2)
         quantise_weights(1)
-        pick(3, True)
-        lay_values(1, True)
-        add_up(0)
-        add_up(1)
-        quantise_values(1)
+        add_up(0, 1)
+        add_up(1, 1)
+        lay_values(slice(2, 4), True)
+        copy_sums(0, True)
+        copy_sums(1, False)
+        quantise_values(slice(2, 4))
+        add_up(2, 0)
+        add_up(2, 1)
+        add_up(3, 0)
+        add_up(3, 1)
         give_out(0, False)
-        add_up(2)
+        copy_sums(2, True)
         give_out(1, False)
-        add_up(3)
+        copy_sums(3, True)
         give_out(2, False)
         give_out(3, True)

@@ -30,6 +30,7 @@ def tile_attend_passedthrough_pickedout_lean_kernel(
     nc = tc.nc
     with ExitStack() as ctx:
         keep = ctx.enter_context(tc.tile_pool(name="keep", bufs=1))
+        shared = ctx.enter_context(tc.tile_pool(name="shared", bufs=1))
         psum = ctx.enter_context(tc.psum_pool(name="psum", bufs=1))
 
         def tiles(name, count, shape, dtype):
@@ -55,12 +56,15 @@ def tile_attend_passedthrough_pickedout_lean_kernel(
         value_banks = {}
         weight_words = {}
         weight_scales = tiles("weight_scales", 2, [P, HALF], U8)
-        value_pool = tiles("value_pool", PLANES, [P, T], F32)
+        value_pool = tiles("value_pool", PLANES - 1, [P, T], F32)
+        value_pool.append(shared.tile([P, T], F32, name="last_value_pool", offset=0, align_bytes=64))
         picked = tiles("picked", PLANES, [P, I], BF16)
-        values_bf = tiles("values_bf", PLANES // 2, [P, 2, P, PACK], BF16)
-        value_words = tiles("value_words", PLANES // 2, [P, 2 * P], U32)
-        value_scales = tiles("value_scales", PLANES // 2, [P, 2 * P], U8)
-        sums = tiles("sums", PLANES, [P, Q], F32)
+        groups = [(0, 1), (2,), (3,)]
+        group_banks = ["mx0", "mx1", "score3"]
+        values_bf = {}
+        value_words = {}
+        value_scales = {}
+        sums = {}
         sum_banks = {}
         result = tiles("result", PLANES, [P, C], F32)
         columns = keep.tile([P, C], F32)
@@ -196,50 +200,57 @@ def tile_attend_passedthrough_pickedout_lean_kernel(
             else:
                 nc.vector.tensor_copy(picked[j][:, cols], window)
 
+        def place_of(j):
+            g = max(j - 1, 0)
+            return g, groups[g].index(j)
+
         def turn_values(j):
+            g, n = place_of(j)
             pairs = picked[j][:].bitcast(F32)
-            if j % 2 == 0:
-                value_banks[j // 2] = psum.tile([P, 2, 2, P], F32, name="value_bank", tag="mx%d" % (j // 2))
+            if n == 0:
+                value_banks[g] = psum.tile([P, len(groups[g]), 2, P], F32, name="value_bank", tag=group_banks[g])
             for u in range(2):
-                nc.tensor.transpose(value_banks[j // 2][:, j % 2, u, :], pairs[:, u::2], identity[:])
+                nc.tensor.transpose(value_banks[g][:, n, u, :], pairs[:, u::2], identity[:])
 
-        def lay_values(planes, on_scalar):
-            g, part = planes.start // 2, slice(planes.start % 2, (planes.stop - 1) % 2 + 1)
-            dst = values_bf[g][:, part].bitcast(F32)
-            src = value_banks[g][:, part].rearrange("p j u e -> p j e u")
-            if on_scalar:
-                nc.scalar.copy(dst, src)
+        def lay_values(g):
+            values_bf[g] = keep.tile([P, len(groups[g]), P, PACK], BF16, name="values_bf%d" % g, align_bytes=64)
+            nc.vector.tensor_copy(values_bf[g][:].bitcast(F32), value_banks[g][:].rearrange("p j u e -> p j e u"))
+
+        def quantise_values(g):
+            width = len(groups[g]) * P
+            if g == 1:
+                value_words[g] = shared.tile([P, width], U32, name="held_words", offset=3 * Q * 4, align_bytes=64)
             else:
-                nc.vector.tensor_copy(dst, src)
-
-        def quantise_values(planes):
-            g, part = planes.start // 2, slice(planes.start % 2, (planes.stop - 1) % 2 + 1)
-            cols = slice(part.start * P, part.stop * P)
+                value_words[g] = keep.tile([P, width], U32, name="value_words%d" % g, align_bytes=64)
+            value_scales[g] = keep.tile([P, width], U8, name="value_scales%d" % g, align_bytes=64)
             nc.vector.quantize_mx(
-                out=value_words[g][:, cols].bitcast(FP8X4),
-                scales=value_scales[g][:, cols],
-                in_=values_bf[g][:, part].rearrange("p j e r -> p (j e r)"),
+                out=value_words[g][:].bitcast(FP8X4),
+                scales=value_scales[g][:],
+                in_=values_bf[g][:].rearrange("p j e r -> p (j e r)"),
             )
 
         def add_up(j, h):
-            cols = slice((j % 2) * P, (j % 2 + 1) * P)
+            g, n = place_of(j)
+            cols = slice(n * P, (n + 1) * P)
             if j not in sum_banks:
                 sum_banks[j] = psum.tile([P, Q], F32, name="sum_bank", tag=["mx2", "mx3", "score0", "score1"][j])
             nc.tensor.matmul_mx(
                 out=sum_banks[j][:, h * HALF : (h + 1) * HALF],
-                lhsT=value_words[j // 2][:, cols].bitcast(FP8X4),
-                lhsT_scale=value_scales[j // 2][:, cols],
+                lhsT=value_words[g][:, cols].bitcast(FP8X4),
+                lhsT_scale=value_scales[g][:, cols],
                 rhs=weight_words[h][:].bitcast(FP8X4),
                 rhs_scale=weight_scales[h][:],
                 start=True,
                 stop=True,
             )
 
-        def copy_sums(j, on_scalar):
-            if on_scalar:
-                nc.scalar.copy(sums[j][:], sum_banks[j][:])
-            else:
-                nc.vector.tensor_copy(sums[j][:], sum_banks[j][:])
+        def copy_sums(j, rows):
+            if j not in sums:
+                if j < PLANES - 1:
+                    sums[j] = shared.tile([P, Q], F32, name="sums%d" % j, offset=j * Q * 4, align_bytes=64)
+                else:
+                    sums[j] = keep.tile([P, Q], F32, name="sums%d" % j, align_bytes=64)
+            nc.scalar.copy(sums[j][:, rows], sum_banks[j][:, rows])
 
         def give_out(j, on_scalar):
             window = sums[j][:].indirect(column_list[:])
@@ -286,29 +297,30 @@ def tile_attend_passedthrough_pickedout_lean_kernel(
         weigh(1)
         pick(2, whole, True)
         turn_values(2)
+        quantise_weights(0)
+        lay_values(0)
+        lay_values(1)
         pick(3, whole, True)
         turn_values(3)
-        quantise_weights(0)
-        lay_values(slice(0, 2), False)
         weigh(3)
-        quantise_values(slice(0, 2))
-        add_up(0, 0)
-        add_up(1, 0)
+        quantise_values(0)
+        quantise_values(1)
+        for j in range(PLANES - 1):
+            add_up(j, 0)
         weigh(2)
+        for j in range(PLANES - 1):
+            copy_sums(j, early)
         quantise_weights(1)
-        add_up(0, 1)
-        add_up(1, 1)
-        lay_values(slice(2, 4), True)
-        copy_sums(0, True)
-        copy_sums(1, False)
-        quantise_values(slice(2, 4))
-        add_up(2, 0)
-        add_up(2, 1)
+        lay_values(2)
+        for j in range(PLANES - 1):
+            add_up(j, 1)
+        quantise_values(2)
+        for j in range(PLANES - 1):
+            copy_sums(j, late)
         add_up(3, 0)
         add_up(3, 1)
         give_out(0, False)
-        copy_sums(2, True)
+        copy_sums(3, whole)
         give_out(1, False)
-        copy_sums(3, True)
         give_out(2, False)
         give_out(3, True)

@@ -56,8 +56,12 @@ def tile_attend_passedthrough_pickedout_lean_kernel(
         value_banks = {}
         weight_words = {}
         weight_scales = tiles("weight_scales", 2, [P, HALF], U8)
-        value_pool = tiles("value_pool", PLANES - 1, [P, T], F32)
-        value_pool.append(shared.tile([P, T], F32, name="last_value_pool", offset=0, align_bytes=64))
+        value_pool = [
+            keep.tile([P, T], F32, name="value_pool0"),
+            shared.tile([P, T], F32, name="value_pool1", offset=T * 4, align_bytes=64),
+            keep.tile([P, T], F32, name="value_pool2"),
+            shared.tile([P, T], F32, name="value_pool3", offset=0, align_bytes=64),
+        ]
         picked = tiles("picked", PLANES, [P, I], BF16)
         groups = [(0, 1), (2,), (3,)]
         group_banks = ["mx0", "mx1", "score3"]
@@ -163,8 +167,10 @@ def tile_attend_passedthrough_pickedout_lean_kernel(
 
         def get(b, on_scalar):
             window = places[b % 2][:].indirect(get_list[:])
-            tag = "value_pool1" if b == 2 else "looked_up%d" % b
-            looked_up[b] = keep.tile([P, I], F32, name="looked_up%d" % b, tag=tag, align_bytes=64)
+            if b < 2:
+                looked_up[b] = keep.tile([P, I], F32, name="looked_up%d" % b)
+            else:
+                looked_up[b] = shared.tile([P, I], F32, name="looked_up%d" % b, offset=(T + (b - 2) * I) * 4, align_bytes=64)
             if on_scalar:
                 nc.scalar.activation(looked_up[b][:], window, COPY)
             else:
@@ -173,8 +179,10 @@ def tile_attend_passedthrough_pickedout_lean_kernel(
 
         def weigh(b):
             if b // 2 not in weights_bf:
-                tag = "products3" if b < 2 else "weights_late"
-                weights_bf[b // 2] = keep.tile([P, 2 * P, PACK], BF16, name="weights_bf", tag=tag, align_bytes=64)
+                if b < 2:
+                    weights_bf[0] = shared.tile([P, 2 * P, PACK], BF16, name="early_bf", offset=(T + 2 * I) * 4, align_bytes=64)
+                else:
+                    weights_bf[1] = keep.tile([P, 2 * P, PACK], BF16, name="late_bf", align_bytes=64)
             nc.vector.scalar_tensor_tensor(
                 out=weights_bf[b // 2][:, (b % 2) * P : (b % 2 + 1) * P, :],
                 in0=score_banks[b][:].rearrange("p r q -> p q r"),
@@ -289,7 +297,7 @@ def tile_attend_passedthrough_pickedout_lean_kernel(
         put_half(2, 0)
         put(3)
         put_half(2, 1)
-        pick(1, whole, True)
+        pick(1, whole, False)
         turn_values(1)
         get(3, False)
         get(2, True)

from contextlib import ExitStack

import concourse.mybir as mybir
from concourse.masks import make_identity

D, T, I, Q, E, Z, C = 512, 2048, 512, 512, 512, 1024, 256
FLOPS = 2 * D * Q * I + 2 * I * E * Q

F32 = mybir.dt.float32
BF16 = mybir.dt.bfloat16
I32 = mybir.dt.int32
U32 = mybir.dt.uint32
U16 = mybir.dt.uint16
U8 = mybir.dt.uint8
FP8X4 = mybir.dt.float8_e4m3fn_x4
COPY = mybir.ActivationFunctionType.Copy
MAX = mybir.AluOpType.max
MULT = mybir.AluOpType.mult

P = 128
PACK = 4
BLOCKS = Q // P
PLANES = E // P
HALF = I // 2


def tile_attend_passedthrough_pickedout_lean_kernel(
    tc, query, keys_words, keys_scales, slot_factor, vals, pgain, offs, offs2, offs3, offs4, out
):
    nc = tc.nc
    with ExitStack() as ctx:
        keep = ctx.enter_context(tc.tile_pool(name="keep", bufs=1))
        shared = ctx.enter_context(tc.tile_pool(name="shared", bufs=1))
        psum = ctx.enter_context(tc.psum_pool(name="psum", bufs=1))

        def tiles(name, count, shape, dtype):
            return [keep.tile(shape, dtype, name="%s%d" % (name, n), tag="%s%d" % (name, n), align_bytes=64) for n in range(count)]

        token_list = keep.tile([P, I // 16], U16)
        put_list = keep.tile([P, I // 16], U16)
        get_list = keep.tile([P, I // 16], U16)
        column_list = keep.tile([P, C // 16], U16)
        pool_words = keep.tile([P, T], U32, align_bytes=64)
        pool_scales = keep.tile([P, T], U8, align_bytes=64)
        key_words = keep.tile([P, I], U32, align_bytes=64)
        key_scales = keep.tile([P, I], U8, align_bytes=64)
        widths = [P, P, 2 * P]
        query_raw = [keep.tile([P, PACK, w], F32, name="query_raw%d" % n) for n, w in enumerate(widths)]
        query_bf = [keep.tile([P, w, PACK], BF16, name="query_bf%d" % n, align_bytes=64) for n, w in enumerate(widths)]
        query_words = [keep.tile([P, w], U32, name="query_words%d" % n, align_bytes=64) for n, w in enumerate(widths)]
        query_scales = [keep.tile([P, w], U8, name="query_scales%d" % n, align_bytes=64) for n, w in enumerate(widths)]
        products = tiles("products", BLOCKS, [P, I], F32)
        places = tiles("places", 2, [P, Z], F32)
        looked_up = {}
        weights_bf = {}
        value_banks = {}
        weight_words = {}
        weight_scales = tiles("weight_scales", 2, [P, HALF], U8)
        value_pool = [
            keep.tile([P, T], F32, name="value_pool0"),
            shared.tile([P, T], F32, name="value_pool1", offset=T * 4, align_bytes=64),
            keep.tile([P, T], F32, name="value_pool2"),
            shared.tile([P, T], F32, name="value_pool3", offset=0, align_bytes=64),
        ]
        picked = tiles("picked", PLANES, [P, I], BF16)
        groups = [(0, 1), (2,), (3,)]
        group_banks = ["mx0", "mx1", "score3"]
        values_bf = {}
        value_words = {}
        value_scales = {}
        sums = {}
        sum_banks = {}
        result = tiles("result", PLANES, [P, C], F32)
        columns = keep.tile([P, C], F32)
        factor = keep.tile([P, PACK], F32)
        gain = keep.tile([P, C], F32)
        identity = keep.tile([P, P], F32, tag="identity", align_bytes=64)

        nc.vector.memset(pool_scales[:].bitcast(I32)[:, 0 : T // 8], 0)
        nc.gpsimd.memset(pool_scales[:].bitcast(I32)[:, T // 8 :], 0)
        for window in places:
            nc.vector.memset(window[:], 0.0)
        make_identity(nc, identity[:])

        query_rows = query.rearrange("(p j) q -> p j q", j=PACK)
        value_rows = vals.rearrange("(p j) t -> p j t", j=PLANES)
        out_rows = out.rearrange("(p j) c -> p j c", j=PLANES)

        nc.sync.dma_start(token_list[:], offs)
        nc.sync.dma_start(query_raw[0][:], query_rows[:, :, 0:P])
        nc.sync.dma_start(put_list[:], offs2)
        for quadrant in range(4):
            nc.sync.dma_start(
                pool_scales[:].bitcast(I32)[32 * quadrant : 32 * quadrant + 4, :],
                keys_scales[0].bitcast(I32)[4 * quadrant : 4 * quadrant + 4, :],
            )
        nc.sync.dma_start(pool_words[:].bitcast(I32), keys_words[0].rearrange("p n r -> p (n r)").bitcast(I32))
        nc.sync.dma_start(query_raw[1][:], query_rows[:, :, P : 2 * P])
        nc.sync.dma_start(query_raw[2][:], query_rows[:, :, 2 * P :])
        nc.sync.dma_start(get_list[:], offs3)
        nc.sync.dma_start(factor[:], slot_factor[0].rearrange("(p r) -> p r", r=PACK))
        for j in range(PLANES):
            nc.sync.dma_start(value_pool[j][:], value_rows[:, j, :])
        nc.sync.dma_start(column_list[:], offs4)
        nc.sync.dma_start(gain[:], pgain[0].partition_broadcast(P))

        def interleave_query(b, on_scalar):
            dst = query_bf[b][:].rearrange("p (c n) r -> p c r n", n=4)
            src = query_raw[b][:].rearrange("p r (c n) -> p c r n", n=4)
            if on_scalar:
                nc.scalar.activation(dst, src, COPY)
            else:
                nc.vector.tensor_copy(dst, src)

        def quantise_query(b):
            nc.vector.quantize_mx(
                out=query_words[b][:].bitcast(FP8X4),
                scales=query_scales[b][:],
                in_=query_bf[b][:].rearrange("p q r -> p (q r)"),
            )

        def gather_keys(h):
            nc.vector.tensor_copy(
                key_words[:, h * HALF : (h + 1) * HALF], pool_words[:].indirect(token_list[:, h * 16 : (h + 1) * 16])
            )

        def score(b, cols, on_scalar, bank_tag):
            bank = psum.tile([P, cols.stop - cols.start], F32, name="product_bank", tag=bank_tag)
            piece = min(b, 2)
            rows = slice((b - piece) * P, (b - piece + 1) * P)
            nc.tensor.matmul_mx(
                out=bank[:],
                lhsT=query_words[piece][:, rows].bitcast(FP8X4),
                lhsT_scale=query_scales[piece][:, rows],
                rhs=key_words[:, cols].bitcast(FP8X4),
                rhs_scale=key_scales[:, cols],
                start=True,
                stop=True,
            )
            if on_scalar:
                nc.scalar.copy(products[b][:, cols], bank[:])
            else:
                nc.vector.tensor_copy(products[b][:, cols], bank[:])

        score_banks = [psum.tile([P, PACK, P], F32, name="score_bank%d" % b, tag="score%d" % b) for b in range(BLOCKS)]

        def turn(b, source, first):
            for r in range(PACK):
                nc.tensor.matmul(
                    score_banks[b][:, r, :],
                    lhsT=source[:, r::PACK],
                    rhs=identity[:],
                    is_transpose=True,
                    start=first and r == 0,
                    stop=not first and r == PACK - 1,
                )

        def put_half(b, h):
            nc.scalar.activation(
                places[b % 2][:].indirect(put_list[:, h * 16 : (h + 1) * 16]),
                products[b][:, h * HALF : (h + 1) * HALF],
                COPY,
            )

        def put(b):
            nc.vector.tensor_copy(places[b % 2][:].indirect(put_list[:]), products[b][:])

        def get(b, on_scalar):
            window = places[b % 2][:].indirect(get_list[:])
            if b < 2:
                looked_up[b] = keep.tile([P, I], F32, name="looked_up%d" % b)
            else:
                looked_up[b] = shared.tile([P, I], F32, name="looked_up%d" % b, offset=(T + (b - 2) * I) * 4, align_bytes=64)
            if on_scalar:
                nc.scalar.activation(looked_up[b][:], window, COPY)
            else:
                nc.vector.tensor_copy(looked_up[b][:], window)
            turn(b, looked_up[b], False)

        def weigh(b):
            if b // 2 not in weights_bf:
                if b < 2:
                    weights_bf[0] = shared.tile([P, 2 * P, PACK], BF16, name="early_bf", offset=(T + 2 * I) * 4, align_bytes=64)
                else:
                    weights_bf[1] = keep.tile([P, 2 * P, PACK], BF16, name="late_bf", align_bytes=64)
            nc.vector.scalar_tensor_tensor(
                out=weights_bf[b // 2][:, (b % 2) * P : (b % 2 + 1) * P, :],
                in0=score_banks[b][:].rearrange("p r q -> p q r"),
                scalar=0.0,
                in1=factor[:].unsqueeze(1).to_broadcast([P, P, PACK]),
                op0=MAX,
                op1=MULT,
            )

        def quantise_weights(h):
            tag = "picked3" if h == 1 else "weight_words"
            weight_words[h] = keep.tile([P, HALF], U32, name="weight_words", tag=tag, align_bytes=64)
            nc.vector.quantize_mx(
                out=weight_words[h][:].bitcast(FP8X4),
                scales=weight_scales[h][:],
                in_=weights_bf[h][:].rearrange("p q r -> p (q r)"),
            )

        def pick(j, cols, on_scalar):
            window = value_pool[j][:].indirect(token_list[:, cols.start // 16 : cols.stop // 16])
            if on_scalar:
                nc.scalar.activation(picked[j][:, cols], window, COPY)
            else:
                nc.vector.tensor_copy(picked[j][:, cols], window)

        def place_of(j):
            g = max(j - 1, 0)
            return g, groups[g].index(j)

        def turn_values(j):
            g, n = place_of(j)
            pairs = picked[j][:].bitcast(F32)
            if n == 0:
                value_banks[g] = psum.tile([P, len(groups[g]), 2, P], F32, name="value_bank", tag=group_banks[g])
            for u in range(2):
                nc.tensor.transpose(value_banks[g][:, n, u, :], pairs[:, u::2], identity[:])

        def lay_values(g):
            values_bf[g] = keep.tile([P, len(groups[g]), P, PACK], BF16, name="values_bf%d" % g, align_bytes=64)
            nc.vector.tensor_copy(values_bf[g][:].bitcast(F32), value_banks[g][:].rearrange("p j u e -> p j e u"))

        def quantise_values(g):
            width = len(groups[g]) * P
            if g == 1:
                value_words[g] = shared.tile([P, width], U32, name="held_words", offset=3 * Q * 4, align_bytes=64)
            else:
                value_words[g] = keep.tile([P, width], U32, name="value_words%d" % g, align_bytes=64)
            value_scales[g] = keep.tile([P, width], U8, name="value_scales%d" % g, align_bytes=64)
            nc.vector.quantize_mx(
                out=value_words[g][:].bitcast(FP8X4),
                scales=value_scales[g][:],
                in_=values_bf[g][:].rearrange("p j e r -> p (j e r)"),
            )

        def add_up(j, h):
            g, n = place_of(j)
            cols = slice(n * P, (n + 1) * P)
            if j not in sum_banks:
                sum_banks[j] = psum.tile([P, Q], F32, name="sum_bank", tag=["mx2", "mx3", "score0", "score1"][j])
            nc.tensor.matmul_mx(
                out=sum_banks[j][:, h * HALF : (h + 1) * HALF],
                lhsT=value_words[g][:, cols].bitcast(FP8X4),
                lhsT_scale=value_scales[g][:, cols],
                rhs=weight_words[h][:].bitcast(FP8X4),
                rhs_scale=weight_scales[h][:],
                start=True,
                stop=True,
            )

        def copy_sums(j, rows):
            if j not in sums:
                if j < PLANES - 1:
                    sums[j] = shared.tile([P, Q], F32, name="sums%d" % j, offset=j * Q * 4, align_bytes=64)
                else:
                    sums[j] = keep.tile([P, Q], F32, name="sums%d" % j, align_bytes=64)
            nc.scalar.copy(sums[j][:, rows], sum_banks[j][:, rows])

        def give_out(j, on_scalar):
            window = sums[j][:].indirect(column_list[:])
            if on_scalar:
                nc.scalar.activation(columns[:], window, COPY)
                nc.vector.tensor_tensor(result[j][:], columns[:], gain[:], MULT)
            else:
                nc.vector.tensor_tensor(result[j][:], window, gain[:], MULT)
            nc.sync.dma_start(out_rows[:, j, :], result[j][:])


        whole, early, late = slice(0, I), slice(0, HALF), slice(HALF, I)
        interleave_query(0, True)
        quantise_query(0)
        nc.vector.tensor_copy(key_scales[:], pool_scales[:].indirect(token_list[:]))
        gather_keys(0)
        score(0, early, True, "mx2")
        gather_keys(1)
        interleave_query(1, True)
        put_half(0, 0)
        score(0, late, True, "mx0")
        quantise_query(1)
        interleave_query(2, False)
        score(1, whole, False, "mx1")
        quantise_query(2)
        score(2, whole, False, "mx2")
        put(1)
        score(3, whole, False, "mx3")
        put_half(0, 1)
        for b in range(BLOCKS):
            turn(b, products[b], True)
        pick(0, whole, True)
        turn_values(0)
        get(0, True)
        get(1, False)
        put_half(2, 0)
        put(3)
        put_half(2, 1)
        pick(1, whole, False)
        turn_values(1)
        get(3, False)
        get(2, True)
        weigh(0)
        weigh(1)
        pick(2, whole, True)
        turn_values(2)
        quantise_weights(0)
        lay_values(0)
        lay_values(1)
        pick(3, whole, True)
        turn_values(3)
        weigh(3)
        quantise_values(0)
        quantise_values(1)
        for j in range(PLANES - 1):
            add_up(j, 0)
        weigh(2)
        for j in range(PLANES - 1):
            copy_sums(j, early)
        quantise_weights(1)
        lay_values(2)
        for j in range(PLANES - 1):
            add_up(j, 1)
        quantise_values(2)
        for j in range(PLANES - 1):
            copy_sums(j, late)
        add_up(3, 0)
        add_up(3, 1)
        give_out(0, False)
        copy_sums(3, whole)
        give_out(1, False)
        give_out(2, False)
        give_out(3, True)
